import numpy as np, ml_dtypes
CORES = [56,61,80,85]
N = 4
import mx_ref
NC, KT, G, WT = 512, 1, 4, 1
C = np.float32(0.043)
BF = ml_dtypes.bfloat16
def cut(t, i, w=512):
    return t[:, w * i:w * i + w]
def tile(rs):
    return np.stack(rs, axis=2).reshape(128, -1).astype(BF)
def layer(w, X):
    out = []
    for i in range(G):
        for t in range(len(X)):
            p = mx_ref.matmul(mx_ref.quantize(cut(w, len(X) * i + t)), X[t])
            z = p if t == 0 else z + p
        out.append(z)
    return out
def act(Z):
    return [np.maximum(z, 0) * C for z in Z]
def setup_inputs(rng):
    def f(*shape):
        return mx_ref.flush((rng.standard_normal(shape, dtype=np.float32) * np.exp2(rng.integers(-2, 3, shape[:-1] + (1,)))).astype(BF))
    return {"x": f(N, 128, KT * 4 * NC), "w1": f(N, 128, G * KT * 512), "w2": f(N, 128, WT * 512)}
def setup_inputs_blocks(rng):
    d = setup_inputs(rng)
    for k in ("x", "w1", "w2"): d[k] = mx_ref.spread(d[k], rng, 4)
    return d
def setup_inputs_wide(rng):
    d = setup_inputs(rng)
    for k in ("x", "w1", "w2"): d[k] = mx_ref.flush((d[k].astype(np.float32) * np.exp2(rng.integers(-8, 9, (N, 1, 1))).astype(np.float32)).astype(BF))
    return d
def setup_inputs_zeros(rng):
    d = setup_inputs(rng); v = d["x"].reshape(N, 128, -1, 4).copy()
    v[np.broadcast_to((rng.random((N, 1, v.shape[2], 1)) < 0.33), v.shape)] = 0
    d["x"] = v.reshape(d["x"].shape)
    return d
def reference(x, w1, w2):
    H = [mx_ref.quantize(tile(act(layer(w1[j], [mx_ref.quantize(cut(x[j], t, 4 * NC)) for t in range(KT)])))) for j in range(N)]
    y = np.zeros((N, 128, N * WT * NC), np.float32)
    for r in range(N):
        for i in range(WT):
            qw = mx_ref.quantize(cut(w2[r], i))
            for j in range(N):
                y[r][:, NC * (WT * j + i):NC * (WT * j + i) + NC] = mx_ref.matmul(qw, H[j])
    return {"y": y}

@@ -1,0 +1,239 @@
+from concourse.bass import DstId, RemoteDMATransfer
+from concourse.mybir import dt, AluOpType, ActivationFunctionType
+
+N = 4
+NC = 512
+G = 4
+CONST = 0.043
+SIM_CORES = 96
+BANK = 512
+NBANKS = 8
+CUTS = (0, 256, 512)
+K = len(CUTS) - 1
+WAY = ("mate", "near")
+FAR_ORDER = (1, 0)
+ACT = {0: "svss"}
+ACT_REST = "svsv"
+
+SCRATCH = {
+    "xb": ("sbuf", [128, 4 * NC], "bfloat16"),
+    "w1b": ("sbuf", [128, 4 * NC], "bfloat16"),
+    "w2b": ("sbuf", [128, 512], "bfloat16"),
+    "xq": ("sbuf", [128, NC], "float8_e4m3fn_x4"),
+    "xs": ("sbuf", [128, NC], "uint8"),
+    "w1q": ("sbuf", [128, NC], "float8_e4m3fn_x4"),
+    "w1s": ("sbuf", [128, NC], "uint8"),
+    "w2q": ("sbuf", [128, 128], "float8_e4m3fn_x4"),
+    "w2s": ("sbuf", [128, 128], "uint8"),
+    "h": ("sbuf", [128, 4 * NC], "bfloat16"),
+    "cq": ("sbuf", [128, N * NC], "float8_e4m3fn_x4"),
+    "cs": ("sbuf", [128, N * NC], "uint8"),
+    "yo": ("sbuf", [128, N * NC], "float32"),
+    "ps": ("psum", [128, NBANKS * BANK], "float32"),
+}
+NPIECES = 2 + 2 * K
+SEMAPHORES = (
+    ["ldx%d" % c for c in range(K)] + ["ldwa", "ldwb", "ldw2"]
+    + ["qx%d" % c for c in range(K)] + ["qwa", "qwb", "qw2"]
+    + ["m1_%d_%d" % (c, b) for c in range(K) for b in range(G)]
+    + ["act%d" % c for c in range(K)] + ["qh%d" % c for c in range(K)]
+    + ["arr%d_%d" % (s, c) for s in range(N) for c in range(K)]
+    + ["m2_%d" % i for i in range(NPIECES)] + ["cp%d" % i for i in range(NPIECES)]
+    + ["st", "sent"]
+)
+
+
+def _count(mask):
+    return bin(mask).count("1")
+
+
+def _plan(T, topo):
+    cores = list(T.cores)
+    ways, roles = {}, {}
+    for s, src in enumerate(cores):
+        far = [d for d in cores if topo.chip(d) != topo.chip(src)]
+        between = [c for c in range(SIM_CORES)
+                   if c not in cores and topo.die(c) == topo.die(src) and topo.may_write(src, c)
+                   and all(topo.may_write(c, d) for d in far)]
+        kinds = {
+            "near": [c for c in between if topo.chip(c) == topo.chip(src)],
+            "mate": [c for c in between if all(topo.mates(topo.chip(c), topo.chip(d)) for d in far)],
+        }
+        leaving = topo.mask(src, kinds["mate"][0])
+        ways[s] = {}
+        for c in range(K):
+            cq_core, cs_core = kinds[WAY[c]][0], kinds[WAY[c]][1]
+            mask = topo.mask(src, cq_core)
+            if topo.chip(cq_core) == topo.chip(src) and mask & ~leaving:
+                mask = mask & ~leaving
+            ways[s][c] = (cq_core, cs_core, mask)
+            roles[cq_core] = (s, c, "q", _count(mask), far)
+            roles[cs_core] = (s, c, "s", _count(mask), far)
+    return ways, roles
+
+
+def _codes(T, a, b):
+    return T.cq[:, a:b].bitcast(dt.uint8)
+
+
+def _plane(T, a, b):
+    return T.cs[:, a:b]
+
+
+def _between(g, core, T, topo, role):
+    s, c, what, announced, far = role
+    a, b = NC * s + CUTS[c], NC * s + CUTS[c + 1]
+    view = _codes(T, a, b) if what == "q" else _plane(T, a, b)
+    mask = topo.mask(core, far[0])
+    for d in far:
+        mask &= topo.mask(core, d)
+    sem = T.sem["arr%d_%d" % (s, c)]
+    g.wait_ge(sem, announced)
+    ids = [DstId(rid=topo.addr(d)[0], pnc=topo.addr(d)[1]) for d in far]
+    g.remote_dma_fused(
+        [RemoteDMATransfer(dst_ids=ids, dma_engine_mask=mask, remote_sem=sem, srcs=[view], dsts=[view for d in far])],
+        local_sem=T.sem.sent)
+    g.wait_ge(T.sem.sent, _count(mask))
+
+
+def rank_program(g, core, T, topo):
+    ways, roles = _plan(T, topo)
+    if core in roles:
+        _between(g, core, T, topo, roles[core])
+        return
+    r = T.rank_of(core)
+    if r is None:
+        return
+    S = T.sem
+    cores = list(T.cores)
+    near = [s for s in range(N) if s != r and topo.chip(cores[s]) == topo.chip(core)]
+    far = [s for s in range(N) if topo.chip(cores[s]) != topo.chip(core)]
+    ten, vec, sca, syn = g.tensor, g.vector, g.scalar, g.sync
+    half = 2 * NC
+
+    def load_x(q, c):
+        q.dma_start(T.xb[:, 4 * CUTS[c]:4 * CUTS[c + 1]], T.x[:, 4 * CUTS[c]:4 * CUTS[c + 1]]).then_inc(S["ldx%d" % c], 16)
+    load_x(syn, 0)
+    sca.dma_start(T.w1b[:, 0:half], T.w1[:, 0:half]).then_inc(S.ldwa, 16)
+    syn.dma_start(T.w1b[:, half:2 * half], T.w1[:, half:2 * half]).then_inc(S.ldwb, 16)
+    for c in range(1, K):
+        load_x(sca if c % 2 else syn, c)
+    syn.dma_start(T.w2b[:], T.w2[:]).then_inc(S.ldw2, 16)
+
+    pieces = [(r, 0, NC, None, 0)]
+    for s in near:
+        pieces.append((s, 0, NC, S["arr%d_0" % s], 2 * _count(topo.mask(cores[s], core))))
+    for c in FAR_ORDER:
+        for s in far:
+            n = sum(_count(topo.mask(w, core)) for w in ways[s][c][:2])
+            pieces.append((s, CUTS[c], CUTS[c + 1], S["arr%d_%d" % (s, c)], n))
+
+    def act_engine(c, b):
+        return ACT.get(c, ACT_REST)[b]
+
+    release = []
+
+    def bank(sem, val):
+        u = len(release)
+        if u >= NBANKS:
+            ten.wait_ge(*release[u - NBANKS])
+        release.append((sem, val))
+        return BANK * (u % NBANKS)
+
+    for c in range(K):
+        a, b_ = CUTS[c], CUTS[c + 1]
+        ten.wait_ge(S["qx%d" % c], 1)
+        for b in range(G):
+            if c == 0 and b == 0:
+                ten.wait_ge(S.qwa, 1)
+            if c == 0 and b == G // 2:
+                ten.wait_ge(S.qwb, 1)
+            p = bank(S["act%d" % c], G)
+            ten.matmul_mx(T.ps[:, p:p + b_ - a], T.w1q[:, 128 * b:128 * b + 128], T.w1s[:, 128 * b:128 * b + 128],
+                          T.xq[:, a:b_], T.xs[:, a:b_], True, True).then_inc(S["m1_%d_%d" % (c, b)], 1)
+    ten.wait_ge(S.qw2, 1)
+    for c in range(K):
+        ten.wait_ge(S["qh%d" % c], 1)
+    where = []
+    for i, (s, a, b_, sem, n) in enumerate(pieces):
+        if sem is not None:
+            ten.wait_ge(sem, n)
+        p = bank(S["cp%d" % i], 1)
+        where.append(p)
+        ten.matmul_mx(T.ps[:, p:p + b_ - a], T.w2q[:], T.w2s[:], T.cq[:, NC * s + a:NC * s + b_],
+                      T.cs[:, NC * s + a:NC * s + b_], True, True).then_inc(S["m2_%d" % i], 1)
+
+    def act(c, b):
+        a, b_ = CUTS[c], CUTS[c + 1]
+        p = BANK * ((G * c + b) % NBANKS)
+        out, src = T.h[:, 4 * a + b:4 * b_:4], T.ps[:, p:p + b_ - a]
+        if act_engine(c, b) == "v":
+            vec.wait_ge(S["m1_%d_%d" % (c, b)], 1)
+            vec.tensor_scalar(out, src, 0.0, CONST, AluOpType.max, AluOpType.mult).then_inc(S["act%d" % c], 1)
+        else:
+            sca.wait_ge(S["m1_%d_%d" % (c, b)], 1)
+            sca.activation(out, src, ActivationFunctionType.Relu, scale=CONST).then_inc(S["act%d" % c], 1)
+
+    def pack_x(c):
+        a, b_ = CUTS[c], CUTS[c + 1]
+        vec.wait_ge(S["ldx%d" % c], 16)
+        vec.quantize_mx(T.xq[:, a:b_], T.xs[:, a:b_], T.xb[:, 4 * a:4 * b_]).then_inc(S["qx%d" % c], 1)
+
+    pack_x(0)
+    vec.wait_ge(S.ldwa, 16)
+    vec.quantize_mx(T.w1q[:, 0:NC // 2], T.w1s[:, 0:NC // 2], T.w1b[:, 0:half]).then_inc(S.qwa, 1)
+    vec.wait_ge(S.ldwb, 16)
+    vec.quantize_mx(T.w1q[:, NC // 2:NC], T.w1s[:, NC // 2:NC], T.w1b[:, half:2 * half]).then_inc(S.qwb, 1)
+    for c in range(K):
+        mine = [b for b in range(G) if act_engine(c, b) == "v"]
+        for k, b in enumerate(mine):
+            act(c, b)
+            if k == 0 and c + 1 < K:
+                pack_x(c + 1)
+        a, b_ = CUTS[c], CUTS[c + 1]
+        vec.wait_ge(S["act%d" % c], G)
+        vec.quantize_mx(T.cq[:, NC * r + a:NC * r + b_], T.cs[:, NC * r + a:NC * r + b_],
+                        T.h[:, 4 * a:4 * b_]).then_inc(S["qh%d" % c], 1)
+    vec.wait_ge(S.ldw2, 16)
+    vec.quantize_mx(T.w2q[:], T.w2s[:], T.w2b[:]).then_inc(S.qw2, 1)
+
+    for c in range(K):
+        for b in range(G):
+            if act_engine(c, b) == "s":
+                act(c, b)
+
+    sent = 0
+    for c in range(K):
+        a, b_ = NC * r + CUTS[c], NC * r + CUTS[c + 1]
+        cq_core, cs_core, mask = ways[r][c]
+        g.wait_ge(S["qh%d" % c], 1)
+        for dst, view in ((cq_core, _codes(T, a, b_)), (cs_core, _plane(T, a, b_))):
+            rid, pid, _se = topo.addr(dst)
+            g.remote_dma(view, view, S["arr%d_%d" % (r, c)], S.sent, pid, rid, mask)
+            sent += _count(mask)
+    for s in near:
+        a, b_ = NC * r, NC * r + NC
+        mask = topo.mask(core, cores[s])
+        rid, pid, _se = topo.addr(cores[s])
+        for view in (_codes(T, a, b_), _plane(T, a, b_)):
+            g.remote_dma(view, view, S["arr%d_0" % r], S.sent, pid, rid, mask)
+            sent += _count(mask)
+
+    syn.wait_ge(S.sent, sent)
+    stores = 0
+    for i, (s, a, b_, sem, n) in enumerate(pieces):
+        p = where[i]
+        out, src = T.yo[:, NC * s + a:NC * s + b_], T.ps[:, p:p + b_ - a]
+        if i % 2 == 0:
+            vec.wait_ge(S["m2_%d" % i], 1)
+            vec.tensor_copy(out, src).then_inc(S["cp%d" % i], 1)
+        else:
+            sca.wait_ge(S["m2_%d" % i], 1)
+            sca.activation(out, src, ActivationFunctionType.Copy).then_inc(S["cp%d" % i], 1)
+        q = syn if (i % 2 == 0 or i < 1 + len(near)) else sca
+        q.wait_ge(S["cp%d" % i], 1)
+        q.dma_start(T.y[:, NC * s + a:NC * s + b_], out).then_inc(S.st, 16)
+        stores += 16
+
+    g.wait_ge(S.sent, sent)
+    g.wait_ge(S.st, stores)

@@ -8,12 +8,13 @@ CONST = 0.043
 SIM_CORES = 96
 BANK = 512
 NBANKS = 8
-CUTS = (0, 256, 512)
+CUTS = (0, 128, 256, 384, 512)
 K = len(CUTS) - 1
-WAY = ("mate", "near")
-FAR_ORDER = (1, 0)
-ACT = {0: "svss"}
-ACT_REST = "svsv"
+WAY = ("near", "mate", "near", "mate")
+SEND_ORDER = (0, 1, 2, 3)
+FAR_ORDER = (0, 1, 2, 3)
+ACT_LAST = "svsv"
+ACT_REST = "svss"
 
 SCRATCH = {
     "xb": ("sbuf", [128, 4 * NC], "bfloat16"),
@@ -37,7 +38,7 @@ SEMAPHORES = (
     + ["qx%d" % c for c in range(K)] + ["qwa", "qwb", "qw2"]
     + ["m1_%d_%d" % (c, b) for c in range(K) for b in range(G)]
     + ["act%d" % c for c in range(K)] + ["qh%d" % c for c in range(K)]
-    + ["arr%d_%d" % (s, c) for s in range(N) for c in range(K)]
+    + ["arr%d_%d" % (s, c) for s in range(N) for c in range(K)] + ["nbr%d" % s for s in range(N)]
     + ["m2_%d" % i for i in range(NPIECES)] + ["cp%d" % i for i in range(NPIECES)]
     + ["st", "sent"]
 )
@@ -61,14 +62,14 @@ def _plan(T, topo):
         }
         leaving = topo.mask(src, kinds["mate"][0])
         ways[s] = {}
-        for c in range(K):
+        for c in SEND_ORDER:
             cq_core, cs_core = kinds[WAY[c]][0], kinds[WAY[c]][1]
             mask = topo.mask(src, cq_core)
             if topo.chip(cq_core) == topo.chip(src) and mask & ~leaving:
                 mask = mask & ~leaving
             ways[s][c] = (cq_core, cs_core, mask)
-            roles[cq_core] = (s, c, "q", _count(mask), far)
-            roles[cs_core] = (s, c, "s", _count(mask), far)
+            roles.setdefault(cq_core, []).append((s, c, "q", _count(mask), far))
+            roles.setdefault(cs_core, []).append((s, c, "s", _count(mask), far))
     return ways, roles
 
 
@@ -80,20 +81,23 @@ def _plane(T, a, b):
     return T.cs[:, a:b]
 
 
-def _between(g, core, T, topo, role):
-    s, c, what, announced, far = role
-    a, b = NC * s + CUTS[c], NC * s + CUTS[c + 1]
-    view = _codes(T, a, b) if what == "q" else _plane(T, a, b)
-    mask = topo.mask(core, far[0])
-    for d in far:
-        mask &= topo.mask(core, d)
-    sem = T.sem["arr%d_%d" % (s, c)]
-    g.wait_ge(sem, announced)
-    ids = [DstId(rid=topo.addr(d)[0], pnc=topo.addr(d)[1]) for d in far]
-    g.remote_dma_fused(
-        [RemoteDMATransfer(dst_ids=ids, dma_engine_mask=mask, remote_sem=sem, srcs=[view], dsts=[view for d in far])],
-        local_sem=T.sem.sent)
-    g.wait_ge(T.sem.sent, _count(mask))
+def _between(g, core, T, topo, todo):
+    sent = 0
+    for s, c, what, announced, far in todo:
+        a, b = NC * s + CUTS[c], NC * s + CUTS[c + 1]
+        view = _codes(T, a, b) if what == "q" else _plane(T, a, b)
+        mask = topo.mask(core, far[0])
+        for d in far:
+            mask &= topo.mask(core, d)
+        sem = T.sem["arr%d_%d" % (s, c)]
+        g.wait_ge(sem, announced)
+        ids = [DstId(rid=topo.addr(d)[0], pnc=topo.addr(d)[1]) for d in far]
+        g.remote_dma_fused(
+            [RemoteDMATransfer(dst_ids=ids, dma_engine_mask=mask, remote_sem=sem, srcs=[view],
+                               dsts=[view for d in far])],
+            local_sem=T.sem.sent)
+        sent += _count(mask)
+    g.wait_ge(T.sem.sent, sent)
 
 
 def rank_program(g, core, T, topo):
@@ -122,14 +126,14 @@ def rank_program(g, core, T, topo):
 
     pieces = [(r, 0, NC, None, 0)]
     for s in near:
-        pieces.append((s, 0, NC, S["arr%d_0" % s], 2 * _count(topo.mask(cores[s], core))))
+        pieces.append((s, 0, NC, S["nbr%d" % s], 2 * _count(topo.mask(cores[s], core))))
     for c in FAR_ORDER:
         for s in far:
             n = sum(_count(topo.mask(w, core)) for w in ways[s][c][:2])
             pieces.append((s, CUTS[c], CUTS[c + 1], S["arr%d_%d" % (s, c)], n))
 
     def act_engine(c, b):
-        return ACT.get(c, ACT_REST)[b]
+        return (ACT_LAST if c == K - 1 else ACT_REST)[b]
 
     release = []
 
@@ -203,7 +207,7 @@ def rank_program(g, core, T, topo):
                 act(c, b)
 
     sent = 0
-    for c in range(K):
+    for c in SEND_ORDER:
         a, b_ = NC * r + CUTS[c], NC * r + CUTS[c + 1]
         cq_core, cs_core, mask = ways[r][c]
         g.wait_ge(S["qh%d" % c], 1)
@@ -216,7 +220,7 @@ def rank_program(g, core, T, topo):
         mask = topo.mask(core, cores[s])
         rid, pid, _se = topo.addr(cores[s])
         for view in (_codes(T, a, b_), _plane(T, a, b_)):
-            g.remote_dma(view, view, S["arr%d_0" % r], S.sent, pid, rid, mask)
+            g.remote_dma(view, view, S["nbr%d" % r], S.sent, pid, rid, mask)
             sent += _count(mask)
 
     syn.wait_ge(S.sent, sent)

from concourse.bass import DstId, RemoteDMATransfer
from concourse.mybir import dt, AluOpType, ActivationFunctionType

N = 4
NC = 512
G = 4
CONST = 0.043
SIM_CORES = 96
BANK = 512
NBANKS = 8
CUTS = (0, 128, 256, 384, 512)
K = len(CUTS) - 1
WAY = ("near", "mate", "near", "mate")
SEND_ORDER = (0, 1, 2, 3)
FAR_ORDER = (0, 1, 2, 3)
ACT_LAST = "svsv"
ACT_REST = "svss"

SCRATCH = {
    "xb": ("sbuf", [128, 4 * NC], "bfloat16"),
    "w1b": ("sbuf", [128, 4 * NC], "bfloat16"),
    "w2b": ("sbuf", [128, 512], "bfloat16"),
    "xq": ("sbuf", [128, NC], "float8_e4m3fn_x4"),
    "xs": ("sbuf", [128, NC], "uint8"),
    "w1q": ("sbuf", [128, NC], "float8_e4m3fn_x4"),
    "w1s": ("sbuf", [128, NC], "uint8"),
    "w2q": ("sbuf", [128, 128], "float8_e4m3fn_x4"),
    "w2s": ("sbuf", [128, 128], "uint8"),
    "h": ("sbuf", [128, 4 * NC], "bfloat16"),
    "cq": ("sbuf", [128, N * NC], "float8_e4m3fn_x4"),
    "cs": ("sbuf", [128, N * NC], "uint8"),
    "yo": ("sbuf", [128, N * NC], "float32"),
    "ps": ("psum", [128, NBANKS * BANK], "float32"),
}
NPIECES = 2 + 2 * K
SEMAPHORES = (
    ["ldx%d" % c for c in range(K)] + ["ldwa", "ldwb", "ldw2"]
    + ["qx%d" % c for c in range(K)] + ["qwa", "qwb", "qw2"]
    + ["m1_%d_%d" % (c, b) for c in range(K) for b in range(G)]
    + ["act%d" % c for c in range(K)] + ["qh%d" % c for c in range(K)]
    + ["arr%d_%d" % (s, c) for s in range(N) for c in range(K)] + ["nbr%d" % s for s in range(N)]
    + ["m2_%d" % i for i in range(NPIECES)] + ["cp%d" % i for i in range(NPIECES)]
    + ["st", "sent"]
)


def _count(mask):
    return bin(mask).count("1")


def _plan(T, topo):
    cores = list(T.cores)
    ways, roles = {}, {}
    for s, src in enumerate(cores):
        far = [d for d in cores if topo.chip(d) != topo.chip(src)]
        between = [c for c in range(SIM_CORES)
                   if c not in cores and topo.die(c) == topo.die(src) and topo.may_write(src, c)
                   and all(topo.may_write(c, d) for d in far)]
        kinds = {
            "near": [c for c in between if topo.chip(c) == topo.chip(src)],
            "mate": [c for c in between if all(topo.mates(topo.chip(c), topo.chip(d)) for d in far)],
        }
        leaving = topo.mask(src, kinds["mate"][0])
        ways[s] = {}
        for c in SEND_ORDER:
            cq_core, cs_core = kinds[WAY[c]][0], kinds[WAY[c]][1]
            mask = topo.mask(src, cq_core)
            if topo.chip(cq_core) == topo.chip(src) and mask & ~leaving:
                mask = mask & ~leaving
            ways[s][c] = (cq_core, cs_core, mask)
            roles.setdefault(cq_core, []).append((s, c, "q", _count(mask), far))
            roles.setdefault(cs_core, []).append((s, c, "s", _count(mask), far))
    return ways, roles


def _codes(T, a, b):
    return T.cq[:, a:b].bitcast(dt.uint8)


def _plane(T, a, b):
    return T.cs[:, a:b]


def _between(g, core, T, topo, todo):
    sent = 0
    for s, c, what, announced, far in todo:
        a, b = NC * s + CUTS[c], NC * s + CUTS[c + 1]
        view = _codes(T, a, b) if what == "q" else _plane(T, a, b)
        mask = topo.mask(core, far[0])
        for d in far:
            mask &= topo.mask(core, d)
        sem = T.sem["arr%d_%d" % (s, c)]
        g.wait_ge(sem, announced)
        ids = [DstId(rid=topo.addr(d)[0], pnc=topo.addr(d)[1]) for d in far]
        g.remote_dma_fused(
            [RemoteDMATransfer(dst_ids=ids, dma_engine_mask=mask, remote_sem=sem, srcs=[view],
                               dsts=[view for d in far])],
            local_sem=T.sem.sent)
        sent += _count(mask)
    g.wait_ge(T.sem.sent, sent)


def rank_program(g, core, T, topo):
    ways, roles = _plan(T, topo)
    if core in roles:
        _between(g, core, T, topo, roles[core])
        return
    r = T.rank_of(core)
    if r is None:
        return
    S = T.sem
    cores = list(T.cores)
    near = [s for s in range(N) if s != r and topo.chip(cores[s]) == topo.chip(core)]
    far = [s for s in range(N) if topo.chip(cores[s]) != topo.chip(core)]
    ten, vec, sca, syn = g.tensor, g.vector, g.scalar, g.sync
    half = 2 * NC

    def load_x(q, c):
        q.dma_start(T.xb[:, 4 * CUTS[c]:4 * CUTS[c + 1]], T.x[:, 4 * CUTS[c]:4 * CUTS[c + 1]]).then_inc(S["ldx%d" % c], 16)
    load_x(syn, 0)
    sca.dma_start(T.w1b[:, 0:half], T.w1[:, 0:half]).then_inc(S.ldwa, 16)
    syn.dma_start(T.w1b[:, half:2 * half], T.w1[:, half:2 * half]).then_inc(S.ldwb, 16)
    for c in range(1, K):
        load_x(sca if c % 2 else syn, c)
    syn.dma_start(T.w2b[:], T.w2[:]).then_inc(S.ldw2, 16)

    pieces = [(r, 0, NC, None, 0)]
    for s in near:
        pieces.append((s, 0, NC, S["nbr%d" % s], 2 * _count(topo.mask(cores[s], core))))
    for c in FAR_ORDER:
        for s in far:
            n = sum(_count(topo.mask(w, core)) for w in ways[s][c][:2])
            pieces.append((s, CUTS[c], CUTS[c + 1], S["arr%d_%d" % (s, c)], n))

    def act_engine(c, b):
        return (ACT_LAST if c == K - 1 else ACT_REST)[b]

    release = []

    def bank(sem, val):
        u = len(release)
        if u >= NBANKS:
            ten.wait_ge(*release[u - NBANKS])
        release.append((sem, val))
        return BANK * (u % NBANKS)

    for c in range(K):
        a, b_ = CUTS[c], CUTS[c + 1]
        ten.wait_ge(S["qx%d" % c], 1)
        for b in range(G):
            if c == 0 and b == 0:
                ten.wait_ge(S.qwa, 1)
            if c == 0 and b == G // 2:
                ten.wait_ge(S.qwb, 1)
            p = bank(S["act%d" % c], G)
            ten.matmul_mx(T.ps[:, p:p + b_ - a], T.w1q[:, 128 * b:128 * b + 128], T.w1s[:, 128 * b:128 * b + 128],
                          T.xq[:, a:b_], T.xs[:, a:b_], True, True).then_inc(S["m1_%d_%d" % (c, b)], 1)
    ten.wait_ge(S.qw2, 1)
    for c in range(K):
        ten.wait_ge(S["qh%d" % c], 1)
    where = []
    for i, (s, a, b_, sem, n) in enumerate(pieces):
        if sem is not None:
            ten.wait_ge(sem, n)
        p = bank(S["cp%d" % i], 1)
        where.append(p)
        ten.matmul_mx(T.ps[:, p:p + b_ - a], T.w2q[:], T.w2s[:], T.cq[:, NC * s + a:NC * s + b_],
                      T.cs[:, NC * s + a:NC * s + b_], True, True).then_inc(S["m2_%d" % i], 1)

    def act(c, b):
        a, b_ = CUTS[c], CUTS[c + 1]
        p = BANK * ((G * c + b) % NBANKS)
        out, src = T.h[:, 4 * a + b:4 * b_:4], T.ps[:, p:p + b_ - a]
        if act_engine(c, b) == "v":
            vec.wait_ge(S["m1_%d_%d" % (c, b)], 1)
            vec.tensor_scalar(out, src, 0.0, CONST, AluOpType.max, AluOpType.mult).then_inc(S["act%d" % c], 1)
        else:
            sca.wait_ge(S["m1_%d_%d" % (c, b)], 1)
            sca.activation(out, src, ActivationFunctionType.Relu, scale=CONST).then_inc(S["act%d" % c], 1)

    def pack_x(c):
        a, b_ = CUTS[c], CUTS[c + 1]
        vec.wait_ge(S["ldx%d" % c], 16)
        vec.quantize_mx(T.xq[:, a:b_], T.xs[:, a:b_], T.xb[:, 4 * a:4 * b_]).then_inc(S["qx%d" % c], 1)

    pack_x(0)
    vec.wait_ge(S.ldwa, 16)
    vec.quantize_mx(T.w1q[:, 0:NC // 2], T.w1s[:, 0:NC // 2], T.w1b[:, 0:half]).then_inc(S.qwa, 1)
    vec.wait_ge(S.ldwb, 16)
    vec.quantize_mx(T.w1q[:, NC // 2:NC], T.w1s[:, NC // 2:NC], T.w1b[:, half:2 * half]).then_inc(S.qwb, 1)
    for c in range(K):
        mine = [b for b in range(G) if act_engine(c, b) == "v"]
        for k, b in enumerate(mine):
            act(c, b)
            if k == 0 and c + 1 < K:
                pack_x(c + 1)
        a, b_ = CUTS[c], CUTS[c + 1]
        vec.wait_ge(S["act%d" % c], G)
        vec.quantize_mx(T.cq[:, NC * r + a:NC * r + b_], T.cs[:, NC * r + a:NC * r + b_],
                        T.h[:, 4 * a:4 * b_]).then_inc(S["qh%d" % c], 1)
    vec.wait_ge(S.ldw2, 16)
    vec.quantize_mx(T.w2q[:], T.w2s[:], T.w2b[:]).then_inc(S.qw2, 1)

    for c in range(K):
        for b in range(G):
            if act_engine(c, b) == "s":
                act(c, b)

    sent = 0
    for c in SEND_ORDER:
        a, b_ = NC * r + CUTS[c], NC * r + CUTS[c + 1]
        cq_core, cs_core, mask = ways[r][c]
        g.wait_ge(S["qh%d" % c], 1)
        for dst, view in ((cq_core, _codes(T, a, b_)), (cs_core, _plane(T, a, b_))):
            rid, pid, _se = topo.addr(dst)
            g.remote_dma(view, view, S["arr%d_%d" % (r, c)], S.sent, pid, rid, mask)
            sent += _count(mask)
    for s in near:
        a, b_ = NC * r, NC * r + NC
        mask = topo.mask(core, cores[s])
        rid, pid, _se = topo.addr(cores[s])
        for view in (_codes(T, a, b_), _plane(T, a, b_)):
            g.remote_dma(view, view, S["nbr%d" % r], S.sent, pid, rid, mask)
            sent += _count(mask)

    syn.wait_ge(S.sent, sent)
    stores = 0
    for i, (s, a, b_, sem, n) in enumerate(pieces):
        p = where[i]
        out, src = T.yo[:, NC * s + a:NC * s + b_], T.ps[:, p:p + b_ - a]
        if i % 2 == 0:
            vec.wait_ge(S["m2_%d" % i], 1)
            vec.tensor_copy(out, src).then_inc(S["cp%d" % i], 1)
        else:
            sca.wait_ge(S["m2_%d" % i], 1)
            sca.activation(out, src, ActivationFunctionType.Copy).then_inc(S["cp%d" % i], 1)
        q = syn if (i % 2 == 0 or i < 1 + len(near)) else sca
        q.wait_ge(S["cp%d" % i], 1)
        q.dma_start(T.y[:, NC * s + a:NC * s + b_], out).then_inc(S.st, 16)
        stores += 16

    g.wait_ge(S.sent, sent)
    g.wait_ge(S.st, stores)
